import numpy as np
import ml_dtypes


def mxq(x, axis, fmt="e4m3"):
    dtype, down = {"e4m3": (ml_dtypes.float8_e4m3fn, 7), "e5m2": (ml_dtypes.float8_e5m2, 14)}[fmt]
    v = np.moveaxis(np.asarray(x, np.float32).astype(ml_dtypes.bfloat16).astype(np.float64), axis, -1)
    blocks = v.reshape(v.shape[:-1] + (-1, 32))
    amax = np.abs(blocks).max(-1, keepdims=True)
    byte = np.maximum(np.where(amax > 0, np.frexp(amax)[1] - 1 + 127, 0) - down, 1)
    scale = np.exp2(byte - 127.0)
    codes = (blocks / scale).astype(np.float32).astype(dtype).astype(np.float64)
    return np.moveaxis((codes * scale).reshape(v.shape), -1, axis)


WIDE = False


def mx_kscale(k):
    if not WIDE:
        return np.ones(k)
    levels = np.array([10, -10, 5, -5, 0])
    if k % 512:
        return np.exp2(np.random.permutation(np.resize(levels, k // 32))).repeat(32)
    a = np.empty((k // 512, 16))
    for p in range(k // 512):
        a[p, :8] = np.random.permutation(np.resize(levels, 8))
        for g in range(8):
            far = levels[np.abs(levels - a[p, g]) >= 10]
            a[p, g + 8] = far[np.random.randint(len(far))]
    return np.exp2(a.ravel()).repeat(32)


def f64(x):
    return np.asarray(x).astype(np.float64)


def striped(idx):
    return np.tile(idx.reshape(-1, 16).T, (8, 1)).astype(np.uint16)


def unstriped(offs):
    return offs[:16].T.reshape(-1).astype(np.int64)


K, T, E, C, N = 512, 2048, 4, 256, 512


def by_expert(wq, xq):
    return np.concatenate([wq[e].T @ xq[:, e * C:(e + 1) * C] for e in range(E)], axis=1)


def setup_inputs():
    n = np.random.standard_normal
    s = mx_kscale(K)[:, None]
    return {
        "xT": (n((K, T)) * s).astype(np.float32),
        "w": (n((E, K, N)) / np.sqrt(K) / s[None]).astype(np.float32),
        "gate": np.tile(np.random.uniform(0.2, 1.0, E * C), (N, 1)).astype(np.float32),
        "offs": striped(np.random.permutation(T)[:E * C]),
    }


def reference(xT, w, gate, offs):
    idx = unstriped(offs)
    xq = mxq(f64(xT)[:, idx], 0, "e4m3")
    y = by_expert(mxq(f64(w), 1, "e4m3"), xq)
    out = np.zeros((N, T))
    out[:, idx] = f64(gate) * y
    return out

@@ -1,0 +1,139 @@
+from contextlib import ExitStack
+
+import concourse.mybir as mybir
+
+K, T, E, C, N = 512, 2048, 4, 256, 512
+FLOPS = 2 * K * N * E * C
+
+F32 = mybir.dt.float32
+BF16 = mybir.dt.bfloat16
+U32 = mybir.dt.uint32
+U16 = mybir.dt.uint16
+U8 = mybir.dt.uint8
+FP8X4 = mybir.dt.float8_e4m3fn_x4
+MULT = mybir.AluOpType.mult
+
+P = 128
+PACK = 4
+HALF = 256
+NB = N // P
+LCOL = C // 16
+
+
+def tile_routed_moe_kernel(tc, xT, w, gate, offs, out):
+    nc = tc.nc
+    with ExitStack() as ctx:
+        lists = ctx.enter_context(tc.tile_pool(name="lists", bufs=1))
+        keep = ctx.enter_context(tc.tile_pool(name="keep", bufs=1))
+        ring = ctx.enter_context(tc.tile_pool(name="ring", bufs=4))
+        psum = ctx.enter_context(tc.psum_pool(name="psum", bufs=8))
+
+        offsets = lists.tile([P, E * C // 16], U16, name="offsets")
+        nc.sync.dma_start(offsets[:], offs)
+
+        xv = xT.rearrange("(p t) n -> p t n", t=PACK)
+        planes = [keep.tile([P, T], F32, name="plane%d" % t) for t in range(PACK)]
+        for t in range(PACK):
+            nc.sync.dma_start(out=planes[t][:], in_=xv[:, t, :])
+
+        wraw = [[keep.tile([P, PACK, HALF], F32, name="wraw%d_%d" % (e, h)) for h in range(2)] for e in range(E)]
+        gates = [keep.tile([P, E * C], F32, name="gate%d" % nb) for nb in range(NB)]
+
+        def load_w(e, h):
+            nc.sync.dma_start(
+                out=wraw[e][h][:],
+                in_=w[e].rearrange("(p j) n -> p j n", j=PACK)[:, :, h * HALF : (h + 1) * HALF],
+            )
+
+        def load_gate(nb):
+            nc.sync.dma_start(out=gates[nb][:], in_=gate[nb * P : (nb + 1) * P, :])
+
+        load_w(0, 0)
+        load_gate(0)
+        load_gate(1)
+        for e in range(1, E):
+            load_w(e, 0)
+        for e in range(E):
+            load_w(e, 1)
+        load_gate(2)
+        load_gate(3)
+
+        wins = [keep.tile([P, T], F32, name="win%d" % nb) for nb in range(NB)]
+        for nb in range(NB):
+            nc.vector.memset(wins[nb][:], 0.0)
+
+        g4 = [keep.tile([P, PACK, 2 * C], F32, name="g4_%d" % u) for u in range(E // 2)]
+        for t in range(PACK - 1):
+            for u in range(E // 2):
+                nc.vector.tensor_copy(
+                    out=g4[u][:, t, :],
+                    in_=planes[t][:].indirect(offsets[:, u * 2 * LCOL : (u + 1) * 2 * LCOL]),
+                )
+        for e in range(E):
+            nc.vector.tensor_copy(
+                out=g4[e // 2][:, PACK - 1, (e % 2) * C : (e % 2 + 1) * C],
+                in_=planes[PACK - 1][:].indirect(offsets[:, e * LCOL : (e + 1) * LCOL]),
+            )
+
+        xg = [keep.tile([P, C * PACK], BF16, name="xg%d" % e, align_bytes=64) for e in range(E)]
+        xc = [keep.tile([P, C], U32, name="xc%d" % e, align_bytes=64) for e in range(E)]
+        xs = [keep.tile([P, C], U8, name="xs%d" % e, align_bytes=64) for e in range(E)]
+        wg = [[keep.tile([P, HALF * PACK], BF16, name="wg%d_%d" % (e, h), align_bytes=64) for h in range(2)] for e in range(E)]
+        wc = [[keep.tile([P, HALF], U32, name="wc%d_%d" % (e, h), align_bytes=64) for h in range(2)] for e in range(E)]
+        ws = [[keep.tile([P, HALF], U8, name="ws%d_%d" % (e, h), align_bytes=64) for h in range(2)] for e in range(E)]
+
+        def prep_scalar(e, h):
+            if h == 0:
+                nc.scalar.copy(
+                    out=xg[e][:].rearrange("p (c t) -> p c t", t=PACK),
+                    in_=g4[e // 2][:, :, (e % 2) * C : (e % 2 + 1) * C].rearrange("p t c -> p c t"),
+                )
+            nc.scalar.copy(
+                out=wg[e][h][:].rearrange("p (n j) -> p n j", j=PACK),
+                in_=wraw[e][h][:].rearrange("p j n -> p n j"),
+            )
+
+        def prep_vector(e, h):
+            if h == 0:
+                nc.vector.quantize_mx(out=xc[e][:].bitcast(FP8X4), scales=xs[e][:], in_=xg[e][:])
+            nc.vector.quantize_mx(out=wc[e][h][:].bitcast(FP8X4), scales=ws[e][h][:], in_=wg[e][h][:])
+
+        def multiply(e, h, b):
+            acc = psum.tile([P, C], F32, name="acc")
+            cols = slice(b * P, (b + 1) * P)
+            nc.tensor.matmul_mx(
+                out=acc[:],
+                lhsT=wc[e][h][:, cols].bitcast(FP8X4),
+                lhsT_scale=ws[e][h][:, cols],
+                rhs=xc[e][:].bitcast(FP8X4),
+                rhs_scale=xs[e][:],
+                start=True,
+                stop=True,
+            )
+            y = ring.tile([P, C], F32, name="y")
+            nc.scalar.copy(out=y[:], in_=acc[:])
+            return y
+
+        def scatter(e, nb, y):
+            nc.vector.tensor_tensor(
+                out=wins[nb][:].indirect(offsets[:, e * LCOL : (e + 1) * LCOL]),
+                in0=y[:],
+                in1=gates[nb][:, e * C : (e + 1) * C],
+                op=MULT,
+            )
+
+        steps = [(e, h) for h in range(2) for e in range(E)]
+        prep_scalar(*steps[0])
+        prep_vector(*steps[0])
+        for i, (e, h) in enumerate(steps):
+            y0 = multiply(e, h, 0)
+            y1 = multiply(e, h, 1)
+            if i + 1 < len(steps):
+                prep_scalar(*steps[i + 1])
+            scatter(e, 2 * h, y0)
+            if i + 1 < len(steps):
+                prep_vector(*steps[i + 1])
+            scatter(e, 2 * h + 1, y1)
+            if e == E - 1:
+                for nb in (2 * h, 2 * h + 1):
+                    nc.sync.dma_start(out=out[nb * P : (nb + 1) * P, :], in_=wins[nb][:])

@@ -60,7 +60,7 @@ def tile_routed_moe_kernel(tc, xT, w, gate, offs, out):
 
         wins = [keep.tile([P, T], F32, name="win%d" % nb) for nb in range(NB)]
         for nb in range(NB):
-            nc.vector.memset(wins[nb][:], 0.0)
+            nc.gpsimd.memset(wins[nb][:], 0.0)
 
         g4 = [keep.tile([P, PACK, 2 * C], F32, name="g4_%d" % u) for u in range(E // 2)]
         for t in range(PACK - 1):
@@ -98,7 +98,8 @@ def tile_routed_moe_kernel(tc, xT, w, gate, offs, out):
                 nc.vector.quantize_mx(out=xc[e][:].bitcast(FP8X4), scales=xs[e][:], in_=xg[e][:])
             nc.vector.quantize_mx(out=wc[e][h][:].bitcast(FP8X4), scales=ws[e][h][:], in_=wg[e][h][:])
 
-        def multiply(e, h, b):
+        def multiply(e, nb):
+            h, b = nb // 2, nb % 2
             acc = psum.tile([P, C], F32, name="acc")
             cols = slice(b * P, (b + 1) * P)
             nc.tensor.matmul_mx(
@@ -112,28 +113,31 @@ def tile_routed_moe_kernel(tc, xT, w, gate, offs, out):
             )
             y = ring.tile([P, C], F32, name="y")
             nc.scalar.copy(out=y[:], in_=acc[:])
-            return y
+            yg = ring.tile([P, C], F32, name="yg")
+            nc.gpsimd.tensor_tensor(out=yg[:], in0=y[:], in1=gates[nb][:, e * C : (e + 1) * C], op=MULT)
+            return yg
 
-        def scatter(e, nb, y):
-            nc.vector.tensor_tensor(
+        def scatter(e, nb, yg):
+            nc.vector.tensor_copy(
                 out=wins[nb][:].indirect(offsets[:, e * LCOL : (e + 1) * LCOL]),
-                in0=y[:],
-                in1=gates[nb][:, e * C : (e + 1) * C],
-                op=MULT,
+                in_=yg[:],
             )
 
-        steps = [(e, h) for h in range(2) for e in range(E)]
-        prep_scalar(*steps[0])
-        prep_vector(*steps[0])
-        for i, (e, h) in enumerate(steps):
-            y0 = multiply(e, h, 0)
-            y1 = multiply(e, h, 1)
-            if i + 1 < len(steps):
-                prep_scalar(*steps[i + 1])
-            scatter(e, 2 * h, y0)
-            if i + 1 < len(steps):
-                prep_vector(*steps[i + 1])
-            scatter(e, 2 * h + 1, y1)
-            if e == E - 1:
-                for nb in (2 * h, 2 * h + 1):
+        units = [(e, nb) for e in range(E) for nb in (0, 1)] + [(e, nb) for nb in (2, 3) for e in range(E)]
+        preps = {}
+        for i, (e, nb) in enumerate(units):
+            preps.setdefault((e, nb // 2), i)
+        need = dict((i, p) for p, i in preps.items())
+        ready = {}
+        for i in range(-3, len(units)):
+            if i + 3 in need:
+                prep_scalar(*need[i + 3])
+            if i + 2 in need:
+                prep_vector(*need[i + 2])
+            if 0 <= i + 1 < len(units):
+                ready[i + 1] = multiply(*units[i + 1])
+            if i >= 0:
+                e, nb = units[i]
+                scatter(e, nb, ready[i])
+                if e == E - 1:
                     nc.sync.dma_start(out=out[nb * P : (nb + 1) * P, :], in_=wins[nb][:])

@@ -25,7 +25,8 @@ def tile_routed_moe_kernel(tc, xT, w, gate, offs, out):
     with ExitStack() as ctx:
         lists = ctx.enter_context(tc.tile_pool(name="lists", bufs=1))
         keep = ctx.enter_context(tc.tile_pool(name="keep", bufs=1))
-        ring = ctx.enter_context(tc.tile_pool(name="ring", bufs=4))
+        ring = ctx.enter_context(tc.tile_pool(name="ring", bufs=10))
+        hold = ctx.enter_context(tc.tile_pool(name="hold", bufs=1))
         psum = ctx.enter_context(tc.psum_pool(name="psum", bufs=8))
 
         offsets = lists.tile([P, E * C // 16], U16, name="offsets")
@@ -36,108 +37,176 @@ def tile_routed_moe_kernel(tc, xT, w, gate, offs, out):
         for t in range(PACK):
             nc.sync.dma_start(out=planes[t][:], in_=xv[:, t, :])
 
-        wraw = [[keep.tile([P, PACK, HALF], F32, name="wraw%d_%d" % (e, h)) for h in range(2)] for e in range(E)]
-        gates = [keep.tile([P, E * C], F32, name="gate%d" % nb) for nb in range(NB)]
+        wraw = [keep.tile([P, PACK, N], F32, name="wraw%d" % e) for e in range(E)]
+        gspan = [(0, 1), (1, 2), (2, 4)]
+        gates = [keep.tile([P, NB, (b - a) * C], F32, name="gate%d" % u) for u, (a, b) in enumerate(gspan)]
+        gv = gate.rearrange("(nb p) j -> p nb j", p=P)
 
-        def load_w(e, h):
+        def load_w(e, f0, f1):
             nc.sync.dma_start(
-                out=wraw[e][h][:],
-                in_=w[e].rearrange("(p j) n -> p j n", j=PACK)[:, :, h * HALF : (h + 1) * HALF],
+                out=wraw[e][:, :, f0:f1],
+                in_=w[e].rearrange("(p j) n -> p j n", j=PACK)[:, :, f0:f1],
             )
 
-        def load_gate(nb):
-            nc.sync.dma_start(out=gates[nb][:], in_=gate[nb * P : (nb + 1) * P, :])
+        def load_gate(u):
+            a, b = gspan[u]
+            nc.sync.dma_start(out=gates[u][:], in_=gv[:, :, a * C : b * C])
 
-        load_w(0, 0)
+        load_w(0, 0, HALF)
         load_gate(0)
+        load_w(0, HALF, N)
+        load_w(1, 0, N)
         load_gate(1)
-        for e in range(1, E):
-            load_w(e, 0)
-        for e in range(E):
-            load_w(e, 1)
+        load_w(2, 0, N)
+        load_w(3, 0, N)
         load_gate(2)
-        load_gate(3)
 
         wins = [keep.tile([P, T], F32, name="win%d" % nb) for nb in range(NB)]
-        for nb in range(NB):
-            nc.gpsimd.memset(wins[nb][:], 0.0)
+        nc.vector.memset(wins[0][:], 0.0)
+        nc.vector.memset(wins[1][:], 0.0)
+        nc.scalar.copy(out=wins[2][:], in_=wins[0][:])
+        nc.scalar.copy(out=wins[3][:], in_=wins[0][:])
 
         g4 = [keep.tile([P, PACK, 2 * C], F32, name="g4_%d" % u) for u in range(E // 2)]
-        for t in range(PACK - 1):
-            for u in range(E // 2):
-                nc.vector.tensor_copy(
-                    out=g4[u][:, t, :],
-                    in_=planes[t][:].indirect(offsets[:, u * 2 * LCOL : (u + 1) * 2 * LCOL]),
-                )
-        for e in range(E):
+
+        def gather(t, s0, s1):
+            u = s0 // 2
             nc.vector.tensor_copy(
-                out=g4[e // 2][:, PACK - 1, (e % 2) * C : (e % 2 + 1) * C],
-                in_=planes[PACK - 1][:].indirect(offsets[:, e * LCOL : (e + 1) * LCOL]),
+                out=g4[u][:, t, (s0 - 2 * u) * C : (s1 - 2 * u) * C],
+                in_=planes[t][:].indirect(offsets[:, s0 * LCOL : s1 * LCOL]),
             )
 
-        xg = [keep.tile([P, C * PACK], BF16, name="xg%d" % e, align_bytes=64) for e in range(E)]
-        xc = [keep.tile([P, C], U32, name="xc%d" % e, align_bytes=64) for e in range(E)]
-        xs = [keep.tile([P, C], U8, name="xs%d" % e, align_bytes=64) for e in range(E)]
-        wg = [[keep.tile([P, HALF * PACK], BF16, name="wg%d_%d" % (e, h), align_bytes=64) for h in range(2)] for e in range(E)]
-        wc = [[keep.tile([P, HALF], U32, name="wc%d_%d" % (e, h), align_bytes=64) for h in range(2)] for e in range(E)]
-        ws = [[keep.tile([P, HALF], U8, name="ws%d_%d" % (e, h), align_bytes=64) for h in range(2)] for e in range(E)]
+        xg = keep.tile([P, E * C * PACK], BF16, name="xg", align_bytes=64)
+        xc = keep.tile([P, E * C], U32, name="xc", align_bytes=64)
+        xs = keep.tile([P, E * C], U8, name="xs", align_bytes=64)
+        stages = []
 
-        def prep_scalar(e, h):
-            if h == 0:
-                nc.scalar.copy(
-                    out=xg[e][:].rearrange("p (c t) -> p c t", t=PACK),
-                    in_=g4[e // 2][:, :, (e % 2) * C : (e % 2 + 1) * C].rearrange("p t c -> p c t"),
-                )
+        def stage(c0, c1, pool, name):
+            stages.append((c0, c1, pool.tile([P, (c1 - c0) * PACK], BF16, name=name, align_bytes=64)))
+
+        def staged(c0, c1):
+            a, t = [(s[0], s[2]) for s in stages if s[0] <= c0 and c1 <= s[1]][0]
+            return t[:, (c0 - a) * PACK : (c1 - a) * PACK]
+
+        wc = keep.tile([P, 2 * E * HALF], U32, name="wc", align_bytes=64)
+        ws = keep.tile([P, 2 * E * HALF], U8, name="ws", align_bytes=64)
+
+        def x_interleave(e):
             nc.scalar.copy(
-                out=wg[e][h][:].rearrange("p (n j) -> p n j", j=PACK),
-                in_=wraw[e][h][:].rearrange("p j n -> p n j"),
+                out=xg[:, e * C * PACK : (e + 1) * C * PACK].rearrange("p (c t) -> p c t", t=PACK),
+                in_=g4[e // 2][:, :, (e % 2) * C : (e % 2 + 1) * C].rearrange("p t c -> p c t"),
             )
 
-        def prep_vector(e, h):
-            if h == 0:
-                nc.vector.quantize_mx(out=xc[e][:].bitcast(FP8X4), scales=xs[e][:], in_=xg[e][:])
-            nc.vector.quantize_mx(out=wc[e][h][:].bitcast(FP8X4), scales=ws[e][h][:], in_=wg[e][h][:])
-
-        def multiply(e, nb):
-            h, b = nb // 2, nb % 2
-            acc = psum.tile([P, C], F32, name="acc")
-            cols = slice(b * P, (b + 1) * P)
-            nc.tensor.matmul_mx(
-                out=acc[:],
-                lhsT=wc[e][h][:, cols].bitcast(FP8X4),
-                lhsT_scale=ws[e][h][:, cols],
-                rhs=xc[e][:].bitcast(FP8X4),
-                rhs_scale=xs[e][:],
-                start=True,
-                stop=True,
+        def x_quantize(s0, s1):
+            nc.vector.quantize_mx(
+                out=xc[:, s0 * C : s1 * C].bitcast(FP8X4),
+                scales=xs[:, s0 * C : s1 * C],
+                in_=xg[:, s0 * C * PACK : s1 * C * PACK],
             )
-            y = ring.tile([P, C], F32, name="y")
+
+        def w_interleave(e, h, f0, f1):
+            c0 = (h * E + e) * HALF
+            nc.scalar.copy(
+                out=staged(c0 + f0, c0 + f1).rearrange("p (n j) -> p n j", j=PACK),
+                in_=wraw[e][:, :, h * HALF + f0 : h * HALF + f1].rearrange("p j n -> p n j"),
+            )
+
+        def w_quantize(c0, c1):
+            nc.vector.quantize_mx(
+                out=wc[:, c0:c1].bitcast(FP8X4),
+                scales=ws[:, c0:c1],
+                in_=staged(c0, c1),
+            )
+
+        def multiply(nb, s0, s1, held=None):
+            if held is None:
+                y = ring.tile([P, (s1 - s0) * C], F32, name="y")
+            else:
+                y = hold.tile([P, (s1 - s0) * C], F32, name=held, align_bytes=64)
+            acc = psum.tile([P, (s1 - s0) * C], F32, name="acc")
+            for e in range(s0, s1):
+                c0 = ((nb // 2) * E + e) * HALF + (nb % 2) * P
+                nc.tensor.matmul_mx(
+                    out=acc[:, (e - s0) * C : (e - s0 + 1) * C],
+                    lhsT=wc[:, c0 : c0 + P].bitcast(FP8X4),
+                    lhsT_scale=ws[:, c0 : c0 + P],
+                    rhs=xc[:, e * C : (e + 1) * C].bitcast(FP8X4),
+                    rhs_scale=xs[:, e * C : (e + 1) * C],
+                    start=True,
+                    stop=True,
+                )
             nc.scalar.copy(out=y[:], in_=acc[:])
-            yg = ring.tile([P, C], F32, name="yg")
-            nc.gpsimd.tensor_tensor(out=yg[:], in0=y[:], in1=gates[nb][:, e * C : (e + 1) * C], op=MULT)
-            return yg
+            return y
 
-        def scatter(e, nb, yg):
-            nc.vector.tensor_copy(
-                out=wins[nb][:].indirect(offsets[:, e * LCOL : (e + 1) * LCOL]),
-                in_=yg[:],
+        def scatter(nb, s0, s1, y):
+            u = min(s0, 2)
+            nc.vector.tensor_tensor(
+                out=wins[nb][:].indirect(offsets[:, s0 * LCOL : s1 * LCOL]),
+                in0=y[:],
+                in1=gates[u][:, nb, :],
+                op=MULT,
             )
 
-        units = [(e, nb) for e in range(E) for nb in (0, 1)] + [(e, nb) for nb in (2, 3) for e in range(E)]
-        preps = {}
-        for i, (e, nb) in enumerate(units):
-            preps.setdefault((e, nb // 2), i)
-        need = dict((i, p) for p, i in preps.items())
-        ready = {}
-        for i in range(-3, len(units)):
-            if i + 3 in need:
-                prep_scalar(*need[i + 3])
-            if i + 2 in need:
-                prep_vector(*need[i + 2])
-            if 0 <= i + 1 < len(units):
-                ready[i + 1] = multiply(*units[i + 1])
-            if i >= 0:
-                e, nb = units[i]
-                scatter(e, nb, ready[i])
-                if e == E - 1:
-                    nc.sync.dma_start(out=out[nb * P : (nb + 1) * P, :], in_=wins[nb][:])
+        def store(nb):
+            nc.sync.dma_start(out=out[nb * P : (nb + 1) * P, :], in_=wins[nb][:])
+
+        stage(0, HALF, keep, "wg00")
+        stage(HALF, 2 * HALF, hold, "holdA")
+        stage(2 * HALF, 4 * HALF, hold, "holdB")
+        stage(E * HALF, (E + 1) * HALF, keep, "wg01")
+        stage((E + 1) * HALF, (E + 2) * HALF, keep, "wg11")
+        stage((E + 2) * HALF, (E + 4) * HALF, keep, "wg231")
+
+        for t in range(PACK - 1):
+            gather(t, 0, 2)
+            gather(t, 2, 4)
+        gather(3, 0, 1)
+        w_interleave(0, 0, 0, P)
+        x_interleave(0)
+        w_quantize(0, P)
+        x_quantize(0, 1)
+        y00 = multiply(0, 0, 1)
+        w_interleave(0, 0, P, HALF)
+        gather(3, 1, 2)
+        w_quantize(P, HALF)
+        y01 = multiply(1, 0, 1)
+        scatter(0, 0, 1, y00)
+        w_interleave(0, 1, 0, HALF)
+        w_quantize(E * HALF, (E + 1) * HALF)
+        y02 = multiply(2, 0, 1)
+        scatter(1, 0, 1, y01)
+        x_interleave(1)
+        gather(3, 2, 3)
+        gather(3, 3, 4)
+        w_interleave(1, 0, 0, HALF)
+        x_quantize(1, 2)
+        w_quantize(HALF, 2 * HALF)
+        w_interleave(1, 1, 0, HALF)
+        w_quantize((E + 1) * HALF, (E + 2) * HALF)
+        scatter(2, 0, 1, y02)
+        x_interleave(2)
+        y03 = multiply(3, 0, 1, "holdA")
+        scatter(3, 0, 1, y03)
+        y10 = multiply(0, 1, 2)
+        y11 = multiply(1, 1, 2)
+        y12 = multiply(2, 1, 2)
+        x_interleave(3)
+        x_quantize(2, 4)
+        scatter(0, 1, 2, y10)
+        w_interleave(2, 0, 0, HALF)
+        w_interleave(3, 0, 0, HALF)
+        w_quantize(2 * HALF, 4 * HALF)
+        scatter(1, 1, 2, y11)
+        w_interleave(2, 1, 0, HALF)
+        w_interleave(3, 1, 0, HALF)
+        w_quantize((E + 2) * HALF, (E + 4) * HALF)
+        scatter(2, 1, 2, y12)
+        y13 = multiply(3, 1, 2, "holdB")
+        scatter(3, 1, 2, y13)
+        y20 = multiply(0, 2, 4)
+        y21 = multiply(1, 2, 4)
+        y22 = multiply(2, 2, 4)
+        y23 = multiply(3, 2, 4)
+        for nb, y in enumerate((y20, y21, y22, y23)):
+            scatter(nb, 2, 4, y)
+            store(nb)

@@ -67,16 +67,32 @@ def tile_routed_moe_kernel(tc, xT, w, gate, offs, out):
         nc.scalar.copy(out=wins[2][:], in_=wins[0][:])
         nc.scalar.copy(out=wins[3][:], in_=wins[0][:])
 
-        g4 = [keep.tile([P, PACK, 2 * C], F32, name="g4_%d" % u) for u in range(E // 2)]
+        g_low = [keep.tile([P, 2, 2 * C], F32, name="g_low%d" % u) for u in range(E // 2)]
+        g_high01 = keep.tile([P, 2, 2 * C], F32, name="g_high01")
+        g_high2 = keep.tile([P, 2, C], F32, name="g_high2")
+        xg0 = keep.tile([P, C * PACK], BF16, name="xg0", align_bytes=64)
+        xg1 = keep.tile([P, C * PACK], BF16, name="xg1", align_bytes=64)
+        xg23 = keep.tile([P, 2 * C * PACK], BF16, name="xg23", align_bytes=64)
+        late = {}
+
+        def gathered(t0, t1, s0, s1):
+            if t0 < 2:
+                return g_low[s0 // 2][:, t0:t1, (s0 % 2) * C : (s0 % 2 + s1 - s0) * C]
+            if s0 < 2:
+                return g_high01[:, t0 - 2 : t1 - 2, s0 * C : s1 * C]
+            return (g_high2 if s0 == 2 else late["g_high3"])[:, t0 - 2 : t1 - 2, :]
 
         def gather(t, s0, s1):
-            u = s0 // 2
             nc.vector.tensor_copy(
-                out=g4[u][:, t, (s0 - 2 * u) * C : (s1 - 2 * u) * C],
+                out=gathered(t, t + 1, s0, s1)[:, 0, :],
                 in_=planes[t][:].indirect(offsets[:, s0 * LCOL : s1 * LCOL]),
             )
 
-        xg = keep.tile([P, E * C * PACK], BF16, name="xg", align_bytes=64)
+        def grouped(s0, s1):
+            if s0 >= 2:
+                return xg23[:, (s0 - 2) * C * PACK : (s1 - 2) * C * PACK]
+            return (xg0 if s0 == 0 else xg1)[:]
+
         xc = keep.tile([P, E * C], U32, name="xc", align_bytes=64)
         xs = keep.tile([P, E * C], U8, name="xs", align_bytes=64)
         stages = []
@@ -91,24 +107,24 @@ def tile_routed_moe_kernel(tc, xT, w, gate, offs, out):
         wc = keep.tile([P, 2 * E * HALF], U32, name="wc", align_bytes=64)
         ws = keep.tile([P, 2 * E * HALF], U8, name="ws", align_bytes=64)
 
-        def x_interleave(e):
+        def x_interleave(e, t0):
             nc.scalar.copy(
-                out=xg[:, e * C * PACK : (e + 1) * C * PACK].rearrange("p (c t) -> p c t", t=PACK),
-                in_=g4[e // 2][:, :, (e % 2) * C : (e % 2 + 1) * C].rearrange("p t c -> p c t"),
+                out=grouped(e, e + 1).rearrange("p (c t) -> p c t", t=PACK)[:, :, t0 : t0 + 2],
+                in_=gathered(t0, t0 + 2, e, e + 1).rearrange("p t c -> p c t"),
             )
 
         def x_quantize(s0, s1):
             nc.vector.quantize_mx(
                 out=xc[:, s0 * C : s1 * C].bitcast(FP8X4),
                 scales=xs[:, s0 * C : s1 * C],
-                in_=xg[:, s0 * C * PACK : s1 * C * PACK],
+                in_=grouped(s0, s1),
             )
 
         def w_interleave(e, h, f0, f1):
             c0 = (h * E + e) * HALF
             nc.scalar.copy(
-                out=staged(c0 + f0, c0 + f1).rearrange("p (n j) -> p n j", j=PACK),
-                in_=wraw[e][:, :, h * HALF + f0 : h * HALF + f1].rearrange("p j n -> p n j"),
+                out=staged(c0 + f0, c0 + f1).rearrange("p (c i j) -> p c j i", i=4, j=PACK),
+                in_=wraw[e][:, :, h * HALF + f0 : h * HALF + f1].rearrange("p j (c i) -> p c j i", i=4),
             )
 
         def w_quantize(c0, c1):
@@ -150,47 +166,53 @@ def tile_routed_moe_kernel(tc, xT, w, gate, offs, out):
         def store(nb):
             nc.sync.dma_start(out=out[nb * P : (nb + 1) * P, :], in_=wins[nb][:])
 
-        stage(0, HALF, keep, "wg00")
+        stage(0, HALF, hold, "holdX")
         stage(HALF, 2 * HALF, hold, "holdA")
         stage(2 * HALF, 4 * HALF, hold, "holdB")
         stage(E * HALF, (E + 1) * HALF, keep, "wg01")
         stage((E + 1) * HALF, (E + 2) * HALF, keep, "wg11")
         stage((E + 2) * HALF, (E + 4) * HALF, keep, "wg231")
 
-        for t in range(PACK - 1):
+        for t in range(2):
             gather(t, 0, 2)
             gather(t, 2, 4)
+        for e in range(E):
+            x_interleave(e, 0)
+        gather(2, 0, 2)
+        gather(2, 2, 3)
         gather(3, 0, 1)
         w_interleave(0, 0, 0, P)
-        x_interleave(0)
+        x_interleave(0, 2)
         w_quantize(0, P)
         x_quantize(0, 1)
         y00 = multiply(0, 0, 1)
         w_interleave(0, 0, P, HALF)
         gather(3, 1, 2)
+        gather(3, 2, 3)
         w_quantize(P, HALF)
         y01 = multiply(1, 0, 1)
+        late["g_high3"] = hold.tile([P, 2, C], F32, name="holdX", align_bytes=64)
+        gather(2, 3, 4)
+        gather(3, 3, 4)
         scatter(0, 0, 1, y00)
         w_interleave(0, 1, 0, HALF)
         w_quantize(E * HALF, (E + 1) * HALF)
         y02 = multiply(2, 0, 1)
         scatter(1, 0, 1, y01)
-        x_interleave(1)
-        gather(3, 2, 3)
-        gather(3, 3, 4)
+        x_interleave(1, 2)
         w_interleave(1, 0, 0, HALF)
         x_quantize(1, 2)
         w_quantize(HALF, 2 * HALF)
         w_interleave(1, 1, 0, HALF)
         w_quantize((E + 1) * HALF, (E + 2) * HALF)
         scatter(2, 0, 1, y02)
-        x_interleave(2)
+        x_interleave(2, 2)
         y03 = multiply(3, 0, 1, "holdA")
         scatter(3, 0, 1, y03)
         y10 = multiply(0, 1, 2)
         y11 = multiply(1, 1, 2)
         y12 = multiply(2, 1, 2)
-        x_interleave(3)
+        x_interleave(3, 2)
         x_quantize(2, 4)
         scatter(0, 1, 2, y10)
         w_interleave(2, 0, 0, HALF)

@@ -52,7 +52,8 @@ def tile_routed_moe_kernel(tc, xT, w, gate, offs, out):
             a, b = gspan[u]
             nc.sync.dma_start(out=gates[u][:], in_=gv[:, :, a * C : b * C])
 
-        load_w(0, 0, HALF)
+        load_w(0, 0, P)
+        load_w(0, P, HALF)
         load_gate(0)
         load_w(0, HALF, N)
         load_w(1, 0, N)
@@ -166,7 +167,8 @@ def tile_routed_moe_kernel(tc, xT, w, gate, offs, out):
         def store(nb):
             nc.sync.dma_start(out=out[nb * P : (nb + 1) * P, :], in_=wins[nb][:])
 
-        stage(0, HALF, hold, "holdX")
+        stage(0, P, hold, "holdX")
+        stage(P, HALF, keep, "wg00b")
         stage(HALF, 2 * HALF, hold, "holdA")
         stage(2 * HALF, 4 * HALF, hold, "holdB")
         stage(E * HALF, (E + 1) * HALF, keep, "wg01")

@@ -54,11 +54,11 @@ def tile_routed_moe_kernel(tc, xT, w, gate, offs, out):
 
         load_w(0, 0, P)
         load_w(0, P, HALF)
-        load_gate(0)
         load_w(0, HALF, N)
+        load_gate(0)
         load_w(1, 0, N)
-        load_gate(1)
         load_w(2, 0, N)
+        load_gate(1)
         load_w(3, 0, N)
         load_gate(2)
 
@@ -68,9 +68,8 @@ def tile_routed_moe_kernel(tc, xT, w, gate, offs, out):
         nc.scalar.copy(out=wins[2][:], in_=wins[0][:])
         nc.scalar.copy(out=wins[3][:], in_=wins[0][:])
 
-        g_low = [keep.tile([P, 2, 2 * C], F32, name="g_low%d" % u) for u in range(E // 2)]
-        g_high01 = keep.tile([P, 2, 2 * C], F32, name="g_high01")
-        g_high2 = keep.tile([P, 2, C], F32, name="g_high2")
+        g_low = keep.tile([P, 2, E * C], F32, name="g_low")
+        g_high = keep.tile([P, 2, 3 * C], F32, name="g_high")
         xg0 = keep.tile([P, C * PACK], BF16, name="xg0", align_bytes=64)
         xg1 = keep.tile([P, C * PACK], BF16, name="xg1", align_bytes=64)
         xg23 = keep.tile([P, 2 * C * PACK], BF16, name="xg23", align_bytes=64)
@@ -78,10 +77,10 @@ def tile_routed_moe_kernel(tc, xT, w, gate, offs, out):
 
         def gathered(t0, t1, s0, s1):
             if t0 < 2:
-                return g_low[s0 // 2][:, t0:t1, (s0 % 2) * C : (s0 % 2 + s1 - s0) * C]
-            if s0 < 2:
-                return g_high01[:, t0 - 2 : t1 - 2, s0 * C : s1 * C]
-            return (g_high2 if s0 == 2 else late["g_high3"])[:, t0 - 2 : t1 - 2, :]
+                return g_low[:, t0:t1, s0 * C : s1 * C]
+            if s0 < 3:
+                return g_high[:, t0 - 2 : t1 - 2, s0 * C : s1 * C]
+            return late["g_high3"][:, t0 - 2 : t1 - 2, :]
 
         def gather(t, s0, s1):
             nc.vector.tensor_copy(
@@ -175,13 +174,12 @@ def tile_routed_moe_kernel(tc, xT, w, gate, offs, out):
         stage((E + 1) * HALF, (E + 2) * HALF, keep, "wg11")
         stage((E + 2) * HALF, (E + 4) * HALF, keep, "wg231")
 
-        for t in range(2):
-            gather(t, 0, 2)
-            gather(t, 2, 4)
+        gather(0, 0, 4)
+        gather(1, 0, 2)
+        gather(1, 2, 4)
         for e in range(E):
             x_interleave(e, 0)
-        gather(2, 0, 2)
-        gather(2, 2, 3)
+        gather(2, 0, 3)
         gather(3, 0, 1)
         w_interleave(0, 0, 0, P)
         x_interleave(0, 2)
@@ -189,8 +187,7 @@ def tile_routed_moe_kernel(tc, xT, w, gate, offs, out):
         x_quantize(0, 1)
         y00 = multiply(0, 0, 1)
         w_interleave(0, 0, P, HALF)
-        gather(3, 1, 2)
-        gather(3, 2, 3)
+        gather(3, 1, 3)
         w_quantize(P, HALF)
         y01 = multiply(1, 0, 1)
         late["g_high3"] = hold.tile([P, 2, C], F32, name="holdX", align_bytes=64)

@@ -48,19 +48,21 @@ def tile_routed_moe_kernel(tc, xT, w, gate, offs, out):
                 in_=w[e].rearrange("(p j) n -> p j n", j=PACK)[:, :, f0:f1],
             )
 
-        def load_gate(u):
+        def load_gate(u, nb0, nb1):
             a, b = gspan[u]
-            nc.sync.dma_start(out=gates[u][:], in_=gv[:, :, a * C : b * C])
+            nc.sync.dma_start(out=gates[u][:, nb0:nb1, :], in_=gv[:, nb0:nb1, a * C : b * C])
 
         load_w(0, 0, P)
         load_w(0, P, HALF)
         load_w(0, HALF, N)
-        load_gate(0)
+        load_gate(0, 0, NB - 1)
         load_w(1, 0, N)
         load_w(2, 0, N)
-        load_gate(1)
+        load_gate(0, NB - 1, NB)
+        load_gate(1, 0, NB - 1)
         load_w(3, 0, N)
-        load_gate(2)
+        load_gate(2, 0, NB)
+        load_gate(1, NB - 1, NB)
 
         wins = [keep.tile([P, T], F32, name="win%d" % nb) for nb in range(NB)]
         nc.vector.memset(wins[0][:], 0.0)
@@ -107,10 +109,11 @@ def tile_routed_moe_kernel(tc, xT, w, gate, offs, out):
         wc = keep.tile([P, 2 * E * HALF], U32, name="wc", align_bytes=64)
         ws = keep.tile([P, 2 * E * HALF], U8, name="ws", align_bytes=64)
 
-        def x_interleave(e, t0):
+        def x_interleave(e, t0, e1=None):
+            e1 = e + 1 if e1 is None else e1
             nc.scalar.copy(
-                out=grouped(e, e + 1).rearrange("p (c t) -> p c t", t=PACK)[:, :, t0 : t0 + 2],
-                in_=gathered(t0, t0 + 2, e, e + 1).rearrange("p t c -> p c t"),
+                out=grouped(e, e1).rearrange("p (c t) -> p c t", t=PACK)[:, :, t0 : t0 + 2],
+                in_=gathered(t0, t0 + 2, e, e1).rearrange("p t c -> p c t"),
             )
 
         def x_quantize(s0, s1):
@@ -168,8 +171,8 @@ def tile_routed_moe_kernel(tc, xT, w, gate, offs, out):
 
         stage(0, P, hold, "holdX")
         stage(P, HALF, keep, "wg00b")
-        stage(HALF, 2 * HALF, hold, "holdA")
-        stage(2 * HALF, 4 * HALF, hold, "holdB")
+        stage(HALF, 2 * HALF, keep, "wg10")
+        stage(2 * HALF, 4 * HALF, keep, "wg230")
         stage(E * HALF, (E + 1) * HALF, keep, "wg01")
         stage((E + 1) * HALF, (E + 2) * HALF, keep, "wg11")
         stage((E + 2) * HALF, (E + 4) * HALF, keep, "wg231")
@@ -177,8 +180,9 @@ def tile_routed_moe_kernel(tc, xT, w, gate, offs, out):
         gather(0, 0, 4)
         gather(1, 0, 2)
         gather(1, 2, 4)
-        for e in range(E):
-            x_interleave(e, 0)
+        x_interleave(0, 0)
+        x_interleave(1, 0)
+        x_interleave(2, 0, 4)
         gather(2, 0, 3)
         gather(3, 0, 1)
         w_interleave(0, 0, 0, P)
@@ -206,7 +210,7 @@ def tile_routed_moe_kernel(tc, xT, w, gate, offs, out):
         w_quantize((E + 1) * HALF, (E + 2) * HALF)
         scatter(2, 0, 1, y02)
         x_interleave(2, 2)
-        y03 = multiply(3, 0, 1, "holdA")
+        y03 = multiply(3, 0, 1)
         scatter(3, 0, 1, y03)
         y10 = multiply(0, 1, 2)
         y11 = multiply(1, 1, 2)
@@ -222,7 +226,7 @@ def tile_routed_moe_kernel(tc, xT, w, gate, offs, out):
         w_interleave(3, 1, 0, HALF)
         w_quantize((E + 2) * HALF, (E + 4) * HALF)
         scatter(2, 1, 2, y12)
-        y13 = multiply(3, 1, 2, "holdB")
+        y13 = multiply(3, 1, 2)
         scatter(3, 1, 2, y13)
         y20 = multiply(0, 2, 4)
         y21 = multiply(1, 2, 4)

@@ -109,9 +109,9 @@ def tile_routed_moe_kernel(tc, xT, w, gate, offs, out):
         wc = keep.tile([P, 2 * E * HALF], U32, name="wc", align_bytes=64)
         ws = keep.tile([P, 2 * E * HALF], U8, name="ws", align_bytes=64)
 
-        def x_interleave(e, t0, e1=None):
+        def x_interleave(e, t0, e1=None, engine=None):
             e1 = e + 1 if e1 is None else e1
-            nc.scalar.copy(
+            (nc.scalar.copy if engine is None else engine.tensor_copy)(
                 out=grouped(e, e1).rearrange("p (c t) -> p c t", t=PACK)[:, :, t0 : t0 + 2],
                 in_=gathered(t0, t0 + 2, e, e1).rearrange("p t c -> p c t"),
             )
@@ -182,7 +182,7 @@ def tile_routed_moe_kernel(tc, xT, w, gate, offs, out):
         gather(1, 2, 4)
         x_interleave(0, 0)
         x_interleave(1, 0)
-        x_interleave(2, 0, 4)
+        x_interleave(2, 0, 4, nc.gpsimd)
         gather(2, 0, 3)
         gather(3, 0, 1)
         w_interleave(0, 0, 0, P)

@@ -178,8 +178,7 @@ def tile_routed_moe_kernel(tc, xT, w, gate, offs, out):
         stage((E + 2) * HALF, (E + 4) * HALF, keep, "wg231")
 
         gather(0, 0, 4)
-        gather(1, 0, 2)
-        gather(1, 2, 4)
+        gather(1, 0, 4)
         x_interleave(0, 0)
         x_interleave(1, 0)
         x_interleave(2, 0, 4, nc.gpsimd)

from contextlib import ExitStack

import concourse.mybir as mybir

K, T, E, C, N = 512, 2048, 4, 256, 512
FLOPS = 2 * K * N * E * C

F32 = mybir.dt.float32
BF16 = mybir.dt.bfloat16
U32 = mybir.dt.uint32
U16 = mybir.dt.uint16
U8 = mybir.dt.uint8
FP8X4 = mybir.dt.float8_e4m3fn_x4
MULT = mybir.AluOpType.mult

P = 128
PACK = 4
HALF = 256
NB = N // P
LCOL = C // 16


def tile_routed_moe_kernel(tc, xT, w, gate, offs, out):
    nc = tc.nc
    with ExitStack() as ctx:
        lists = ctx.enter_context(tc.tile_pool(name="lists", bufs=1))
        keep = ctx.enter_context(tc.tile_pool(name="keep", bufs=1))
        ring = ctx.enter_context(tc.tile_pool(name="ring", bufs=10))
        hold = ctx.enter_context(tc.tile_pool(name="hold", bufs=1))
        psum = ctx.enter_context(tc.psum_pool(name="psum", bufs=8))

        offsets = lists.tile([P, E * C // 16], U16, name="offsets")
        nc.sync.dma_start(offsets[:], offs)

        xv = xT.rearrange("(p t) n -> p t n", t=PACK)
        planes = [keep.tile([P, T], F32, name="plane%d" % t) for t in range(PACK)]
        for t in range(PACK):
            nc.sync.dma_start(out=planes[t][:], in_=xv[:, t, :])

        wraw = [keep.tile([P, PACK, N], F32, name="wraw%d" % e) for e in range(E)]
        gspan = [(0, 1), (1, 2), (2, 4)]
        gates = [keep.tile([P, NB, (b - a) * C], F32, name="gate%d" % u) for u, (a, b) in enumerate(gspan)]
        gv = gate.rearrange("(nb p) j -> p nb j", p=P)

        def load_w(e, f0, f1):
            nc.sync.dma_start(
                out=wraw[e][:, :, f0:f1],
                in_=w[e].rearrange("(p j) n -> p j n", j=PACK)[:, :, f0:f1],
            )

        def load_gate(u, nb0, nb1):
            a, b = gspan[u]
            nc.sync.dma_start(out=gates[u][:, nb0:nb1, :], in_=gv[:, nb0:nb1, a * C : b * C])

        load_w(0, 0, P)
        load_w(0, P, HALF)
        load_w(0, HALF, N)
        load_gate(0, 0, NB - 1)
        load_w(1, 0, N)
        load_w(2, 0, N)
        load_gate(0, NB - 1, NB)
        load_gate(1, 0, NB - 1)
        load_w(3, 0, N)
        load_gate(2, 0, NB)
        load_gate(1, NB - 1, NB)

        wins = [keep.tile([P, T], F32, name="win%d" % nb) for nb in range(NB)]
        nc.vector.memset(wins[0][:], 0.0)
        nc.vector.memset(wins[1][:], 0.0)
        nc.scalar.copy(out=wins[2][:], in_=wins[0][:])
        nc.scalar.copy(out=wins[3][:], in_=wins[0][:])

        g_low = keep.tile([P, 2, E * C], F32, name="g_low")
        g_high = keep.tile([P, 2, 3 * C], F32, name="g_high")
        xg0 = keep.tile([P, C * PACK], BF16, name="xg0", align_bytes=64)
        xg1 = keep.tile([P, C * PACK], BF16, name="xg1", align_bytes=64)
        xg23 = keep.tile([P, 2 * C * PACK], BF16, name="xg23", align_bytes=64)
        late = {}

        def gathered(t0, t1, s0, s1):
            if t0 < 2:
                return g_low[:, t0:t1, s0 * C : s1 * C]
            if s0 < 3:
                return g_high[:, t0 - 2 : t1 - 2, s0 * C : s1 * C]
            return late["g_high3"][:, t0 - 2 : t1 - 2, :]

        def gather(t, s0, s1):
            nc.vector.tensor_copy(
                out=gathered(t, t + 1, s0, s1)[:, 0, :],
                in_=planes[t][:].indirect(offsets[:, s0 * LCOL : s1 * LCOL]),
            )

        def grouped(s0, s1):
            if s0 >= 2:
                return xg23[:, (s0 - 2) * C * PACK : (s1 - 2) * C * PACK]
            return (xg0 if s0 == 0 else xg1)[:]

        xc = keep.tile([P, E * C], U32, name="xc", align_bytes=64)
        xs = keep.tile([P, E * C], U8, name="xs", align_bytes=64)
        stages = []

        def stage(c0, c1, pool, name):
            stages.append((c0, c1, pool.tile([P, (c1 - c0) * PACK], BF16, name=name, align_bytes=64)))

        def staged(c0, c1):
            a, t = [(s[0], s[2]) for s in stages if s[0] <= c0 and c1 <= s[1]][0]
            return t[:, (c0 - a) * PACK : (c1 - a) * PACK]

        wc = keep.tile([P, 2 * E * HALF], U32, name="wc", align_bytes=64)
        ws = keep.tile([P, 2 * E * HALF], U8, name="ws", align_bytes=64)

        def x_interleave(e, t0, e1=None, engine=None):
            e1 = e + 1 if e1 is None else e1
            (nc.scalar.copy if engine is None else engine.tensor_copy)(
                out=grouped(e, e1).rearrange("p (c t) -> p c t", t=PACK)[:, :, t0 : t0 + 2],
                in_=gathered(t0, t0 + 2, e, e1).rearrange("p t c -> p c t"),
            )

        def x_quantize(s0, s1):
            nc.vector.quantize_mx(
                out=xc[:, s0 * C : s1 * C].bitcast(FP8X4),
                scales=xs[:, s0 * C : s1 * C],
                in_=grouped(s0, s1),
            )

        def w_interleave(e, h, f0, f1):
            c0 = (h * E + e) * HALF
            nc.scalar.copy(
                out=staged(c0 + f0, c0 + f1).rearrange("p (c i j) -> p c j i", i=4, j=PACK),
                in_=wraw[e][:, :, h * HALF + f0 : h * HALF + f1].rearrange("p j (c i) -> p c j i", i=4),
            )

        def w_quantize(c0, c1):
            nc.vector.quantize_mx(
                out=wc[:, c0:c1].bitcast(FP8X4),
                scales=ws[:, c0:c1],
                in_=staged(c0, c1),
            )

        def multiply(nb, s0, s1, held=None):
            if held is None:
                y = ring.tile([P, (s1 - s0) * C], F32, name="y")
            else:
                y = hold.tile([P, (s1 - s0) * C], F32, name=held, align_bytes=64)
            acc = psum.tile([P, (s1 - s0) * C], F32, name="acc")
            for e in range(s0, s1):
                c0 = ((nb // 2) * E + e) * HALF + (nb % 2) * P
                nc.tensor.matmul_mx(
                    out=acc[:, (e - s0) * C : (e - s0 + 1) * C],
                    lhsT=wc[:, c0 : c0 + P].bitcast(FP8X4),
                    lhsT_scale=ws[:, c0 : c0 + P],
                    rhs=xc[:, e * C : (e + 1) * C].bitcast(FP8X4),
                    rhs_scale=xs[:, e * C : (e + 1) * C],
                    start=True,
                    stop=True,
                )
            nc.scalar.copy(out=y[:], in_=acc[:])
            return y

        def scatter(nb, s0, s1, y):
            u = min(s0, 2)
            nc.vector.tensor_tensor(
                out=wins[nb][:].indirect(offsets[:, s0 * LCOL : s1 * LCOL]),
                in0=y[:],
                in1=gates[u][:, nb, :],
                op=MULT,
            )

        def store(nb):
            nc.sync.dma_start(out=out[nb * P : (nb + 1) * P, :], in_=wins[nb][:])

        stage(0, P, hold, "holdX")
        stage(P, HALF, keep, "wg00b")
        stage(HALF, 2 * HALF, keep, "wg10")
        stage(2 * HALF, 4 * HALF, keep, "wg230")
        stage(E * HALF, (E + 1) * HALF, keep, "wg01")
        stage((E + 1) * HALF, (E + 2) * HALF, keep, "wg11")
        stage((E + 2) * HALF, (E + 4) * HALF, keep, "wg231")

        gather(0, 0, 4)
        gather(1, 0, 4)
        x_interleave(0, 0)
        x_interleave(1, 0)
        x_interleave(2, 0, 4, nc.gpsimd)
        gather(2, 0, 3)
        gather(3, 0, 1)
        w_interleave(0, 0, 0, P)
        x_interleave(0, 2)
        w_quantize(0, P)
        x_quantize(0, 1)
        y00 = multiply(0, 0, 1)
        w_interleave(0, 0, P, HALF)
        gather(3, 1, 3)
        w_quantize(P, HALF)
        y01 = multiply(1, 0, 1)
        late["g_high3"] = hold.tile([P, 2, C], F32, name="holdX", align_bytes=64)
        gather(2, 3, 4)
        gather(3, 3, 4)
        scatter(0, 0, 1, y00)
        w_interleave(0, 1, 0, HALF)
        w_quantize(E * HALF, (E + 1) * HALF)
        y02 = multiply(2, 0, 1)
        scatter(1, 0, 1, y01)
        x_interleave(1, 2)
        w_interleave(1, 0, 0, HALF)
        x_quantize(1, 2)
        w_quantize(HALF, 2 * HALF)
        w_interleave(1, 1, 0, HALF)
        w_quantize((E + 1) * HALF, (E + 2) * HALF)
        scatter(2, 0, 1, y02)
        x_interleave(2, 2)
        y03 = multiply(3, 0, 1)
        scatter(3, 0, 1, y03)
        y10 = multiply(0, 1, 2)
        y11 = multiply(1, 1, 2)
        y12 = multiply(2, 1, 2)
        x_interleave(3, 2)
        x_quantize(2, 4)
        scatter(0, 1, 2, y10)
        w_interleave(2, 0, 0, HALF)
        w_interleave(3, 0, 0, HALF)
        w_quantize(2 * HALF, 4 * HALF)
        scatter(1, 1, 2, y11)
        w_interleave(2, 1, 0, HALF)
        w_interleave(3, 1, 0, HALF)
        w_quantize((E + 2) * HALF, (E + 4) * HALF)
        scatter(2, 1, 2, y12)
        y13 = multiply(3, 1, 2)
        scatter(3, 1, 2, y13)
        y20 = multiply(0, 2, 4)
        y21 = multiply(1, 2, 4)
        y22 = multiply(2, 2, 4)
        y23 = multiply(3, 2, 4)
        for nb, y in enumerate((y20, y21, y22, y23)):
            scatter(nb, 2, 4, y)
            store(nb)
